import numpy as np
import ml_dtypes


def mxq(x, axis, fmt="e4m3"):
    dtype, down = {"e4m3": (ml_dtypes.float8_e4m3fn, 7), "e5m2": (ml_dtypes.float8_e5m2, 14)}[fmt]
    v = np.moveaxis(np.asarray(x, np.float32).astype(ml_dtypes.bfloat16).astype(np.float64), axis, -1)
    blocks = v.reshape(v.shape[:-1] + (-1, 32))
    amax = np.abs(blocks).max(-1, keepdims=True)
    byte = np.maximum(np.where(amax > 0, np.frexp(amax)[1] - 1 + 127, 0) - down, 1)
    scale = np.exp2(byte - 127.0)
    codes = (blocks / scale).astype(np.float32).astype(dtype).astype(np.float64)
    return np.moveaxis((codes * scale).reshape(v.shape), -1, axis)


WIDE = False


def mx_kscale(k):
    if not WIDE:
        return np.ones(k)
    levels = np.array([10, -10, 5, -5, 0])
    if k % 512:
        return np.exp2(np.random.permutation(np.resize(levels, k // 32))).repeat(32)
    a = np.empty((k // 512, 16))
    for p in range(k // 512):
        a[p, :8] = np.random.permutation(np.resize(levels, 8))
        for g in range(8):
            far = levels[np.abs(levels - a[p, g]) >= 10]
            a[p, g + 8] = far[np.random.randint(len(far))]
    return np.exp2(a.ravel()).repeat(32)


def f64(x):
    return np.asarray(x).astype(np.float64)


def striped(idx):
    return np.tile(idx.reshape(-1, 16).T, (8, 1)).astype(np.uint16)


def unstriped(offs):
    return offs[:16].T.reshape(-1).astype(np.int64)


def gelu(v):
    return 0.5 * v * (1.0 + np.tanh(np.sqrt(2.0 / np.pi) * (v + 0.044715 * v**3)))


K, T, D, S, V, H, N = 512, 2048, 4, 1024, 512, 512, 256


def setup_inputs():
    n = np.random.standard_normal
    s = mx_kscale(K)[:, None]
    u = mx_kscale(H)
    return {
        "xT": (n((K, T)) * s).astype(np.float32),
        "w1": (n((K, H)) / np.sqrt(K) / s * u).astype(np.float32),
        "w2": (n((H, N)) / np.sqrt(H) / u[:, None]).astype(np.float32),
        "gate": np.tile(np.random.uniform(0.2, 1.0, (D, 1, V)) / np.sqrt(D), (1, N, 1)).astype(np.float32),
        "offs": striped(np.random.permutation(T)[:S]),
        "pos1": striped(np.random.permutation(S)[:V]),
        "pos2": striped(np.random.permutation(S)[:V]),
        "pos3": striped(np.random.permutation(S)[:V]),
        "pos4": striped(np.random.permutation(S)[:V]),
    }


def reference(xT, w1, w2, gate, offs, pos1, pos2, pos3, pos4):
    idx = unstriped(offs)
    xq = mxq(f64(xT)[:, idx], 0, "e4m3")
    h = gelu(mxq(f64(w1), 0, "e4m3").T @ xq)
    y = mxq(f64(w2), 0, "e4m3").T @ mxq(h, 0, "e4m3")
    return sum(f64(gate[d]) * y[:, unstriped(p)] for d, p in enumerate((pos1, pos2, pos3, pos4)))

@@ -1,0 +1,183 @@
+from contextlib import ExitStack
+
+import concourse.mybir as mybir
+
+K, T, D, S, V, H, N = 512, 2048, 4, 1024, 512, 512, 256
+FLOPS = 2 * S * (K * H + H * N) + 2 * D * N * V
+
+F32 = mybir.dt.float32
+BF16 = mybir.dt.bfloat16
+U32 = mybir.dt.uint32
+U16 = mybir.dt.uint16
+U8 = mybir.dt.uint8
+FP8X4 = mybir.dt.float8_e4m3fn_x4
+COPY = mybir.ActivationFunctionType.Copy
+GELU = mybir.ActivationFunctionType.Gelu_apprx_tanh
+MULT = mybir.AluOpType.mult
+ADD = mybir.AluOpType.add
+
+P = 128
+SLICE = 256
+
+
+def tile_picked_sub_mlp_gelu_sub_e_kernel(tc, xT, w1, w2, gate, offs, pos1, pos2, pos3, pos4, out):
+    nc = tc.nc
+    with ExitStack() as ctx:
+        keep = ctx.enter_context(tc.tile_pool(name="keep", bufs=1))
+        psum_h = ctx.enter_context(tc.psum_pool(name="psum_h", bufs=4))
+        psum_y = ctx.enter_context(tc.psum_pool(name="psum_y", bufs=1))
+
+        warm = keep.tile([P, 1], F32, name="warm")
+        nc.vector.memset(warm[:], 0.0)
+        nc.scalar.activation(out=warm[:], in_=warm[:], func=GELU)
+
+        w1_raw = keep.tile([P, 4, H], F32, name="w1_raw")
+        w2_raw = keep.tile([P, 4, N], F32, name="w2_raw")
+        x_view = xT.rearrange("(p u e) t -> u p e t", u=2, e=2)
+        chunks = ((0, 1024), (1024, 1024)), ((0, 1024), (1024, 512), (1536, 512))
+        raws = []
+        offs_sb = keep.tile([P, S // 16], U16, name="offs_sb")
+        nc.sync.dma_start(offs_sb[:], offs)
+        nc.sync.dma_start(out=w1_raw[:], in_=w1.rearrange("(p j) c -> p j c", j=4))
+        for u in range(2):
+            for c0, n in chunks[u]:
+                raw = keep.tile([P, 2, n], F32, name=f"x_raw_{u}_{c0}")
+                nc.sync.dma_start(out=raw[:], in_=x_view[u, :, :, c0 : c0 + n])
+                raws.append((u, c0, n, raw))
+        nc.sync.dma_start(out=w2_raw[:], in_=w2.rearrange("(p j) c -> p j c", j=4))
+        pos_sb = []
+        for d, pos in enumerate((pos1, pos2, pos3, pos4)):
+            t = keep.tile([P, V // 16], U16, name=f"pos_sb_{d}")
+            nc.sync.dma_start(t[:], pos)
+            pos_sb.append(t)
+        gates = []
+        for b in range(2):
+            t = keep.tile([P, D, V], F32, name=f"gate_sb_{b}")
+            nc.sync.dma_start(out=t[:], in_=gate[:, b * P : (b + 1) * P, :].rearrange("d p v -> p d v"))
+            gates.append(t)
+
+        w1_bf = keep.tile([P, 4, P, 4], BF16, align_bytes=64, name="w1_bf")
+        w1_q = keep.tile([P, H], U32, align_bytes=64, name="w1_q")
+        w1_s = keep.tile([P, H], U8, align_bytes=64, name="w1_s")
+        nc.vector.tensor_copy(out=w1_bf[:], in_=w1_raw[:].rearrange("p j (m t) -> p t m j", t=4))
+        nc.vector.quantize_mx(out=w1_q[:].bitcast(FP8X4), scales=w1_s[:], in_=w1_bf[:].rearrange("p t m j -> p (t m j)"))
+
+        pairs = [keep.tile([P, T, 2], BF16, align_bytes=64, name=f"pair_{u}") for u in range(2)]
+        picked = [keep.tile([P, SLICE, 4], BF16, align_bytes=64, name=f"picked_{i}") for i in range(S // SLICE)]
+
+        def cast(engine, u, c0, raw, a, b):
+            o = pairs[u][:, c0 + a : c0 + b, :]
+            i = raw[:, :, a:b].rearrange("p e t -> p t e")
+            if engine == "v":
+                nc.vector.tensor_copy(out=o, in_=i)
+            else:
+                nc.scalar.activation(out=o, in_=i, func=COPY)
+
+        def gather(u, i):
+            words = picked[i][:].rearrange("p n k -> p (n k)").bitcast(U32).rearrange("p (n u) -> p n u", u=2)
+            window = pairs[u][:].rearrange("p t e -> p (t e)").bitcast(U32)
+            cols = SLICE // 16
+            nc.vector.tensor_copy(out=words[:, :, u], in_=window.indirect(offs_sb[:, i * cols : (i + 1) * cols]))
+
+        for u, c0, n, raw in raws:
+            v_share = 384 if n == 1024 else (128 if c0 == 1024 else 320)
+            cast("s", u, c0, raw, v_share, n)
+            cast("v", u, c0, raw, 0, v_share)
+            if u == 0 and c0 + n == T:
+                for i in range(S // SLICE):
+                    gather(0, i)
+
+        x_q = [keep.tile([P, SLICE], U32, align_bytes=64, name=f"x_q_{i}") for i in range(S // SLICE)]
+        x_s = [keep.tile([P, SLICE], U8, align_bytes=64, name=f"x_s_{i}") for i in range(S // SLICE)]
+        h_bf = [keep.tile([P, SLICE, 4], BF16, align_bytes=64, name=f"h_bf_{i}") for i in range(S // SLICE)]
+        h_q = [keep.tile([P, SLICE], U32, align_bytes=64, name=f"h_q_{i}") for i in range(S // SLICE)]
+        h_s = [keep.tile([P, SLICE], U8, align_bytes=64, name=f"h_s_{i}") for i in range(S // SLICE)]
+        w2_bf = keep.tile([P, N, 4], BF16, align_bytes=64, name="w2_bf")
+        w2_q = keep.tile([P, N], U32, align_bytes=64, name="w2_q")
+        w2_s = keep.tile([P, N], U8, align_bytes=64, name="w2_s")
+        y_ps = [[psum_y.tile([P, 512], F32, name=f"y_ps_{b}_{i}") for i in range(2)] for b in range(2)]
+        y_sb = [keep.tile([P, S], F32, name=f"y_sb_{b}") for b in range(2)]
+
+        def quant_x(i):
+            nc.vector.quantize_mx(out=x_q[i][:].bitcast(FP8X4), scales=x_s[i][:], in_=picked[i][:].rearrange("p n k -> p (n k)"))
+
+        def layer1(i):
+            for half in range(SLICE // P):
+                cols = slice(half * P, (half + 1) * P)
+                ps = psum_h.tile([P, 4, P], F32, name="ps_h")
+                for t in range(4):
+                    nc.tensor.matmul_mx(
+                        out=ps[:, t, :],
+                        lhsT=w1_q[:, t * P : (t + 1) * P].bitcast(FP8X4),
+                        lhsT_scale=w1_s[:, t * P : (t + 1) * P],
+                        rhs=x_q[i][:, cols].bitcast(FP8X4),
+                        rhs_scale=x_s[i][:, cols],
+                        start=True,
+                        stop=True,
+                    )
+                nc.scalar.activation(out=h_bf[i][:, cols, :], in_=ps[:].rearrange("p t n -> p n t"), func=GELU)
+
+        def quant_h(i, a, b):
+            nc.vector.quantize_mx(
+                out=h_q[i][:, a:b].bitcast(FP8X4), scales=h_s[i][:, a:b], in_=h_bf[i][:, a:b, :].rearrange("p n k -> p (n k)")
+            )
+
+        def layer2(i, a, b):
+            for m in range(2):
+                c = (i % 2) * SLICE
+                nc.tensor.matmul_mx(
+                    out=y_ps[m][i // 2][:, c + a : c + b],
+                    lhsT=w2_q[:, m * P : (m + 1) * P].bitcast(FP8X4),
+                    lhsT_scale=w2_s[:, m * P : (m + 1) * P],
+                    rhs=h_q[i][:, a:b].bitcast(FP8X4),
+                    rhs_scale=h_s[i][:, a:b],
+                    start=True,
+                    stop=True,
+                )
+
+        def y_out(engine, m, a, b):
+            o, i = y_sb[m][:, a:b], y_ps[m][a // 512][:, a % 512 : (b - 1) % 512 + 1]
+            if engine == "v":
+                nc.vector.tensor_copy(out=o, in_=i)
+            else:
+                nc.scalar.activation(out=o, in_=i, func=COPY)
+
+        gather(1, 0)
+        quant_x(0)
+        layer1(0)
+        gather(1, 1)
+        quant_x(1)
+        layer1(1)
+        nc.vector.tensor_copy(out=w2_bf[:], in_=w2_raw[:].rearrange("p j c -> p c j"))
+        nc.vector.quantize_mx(out=w2_q[:].bitcast(FP8X4), scales=w2_s[:], in_=w2_bf[:].rearrange("p c j -> p (c j)"))
+        gather(1, 2)
+        quant_x(2)
+        layer1(2)
+        quant_h(0, 0, 256)
+        layer2(0, 0, 256)
+        gather(1, 3)
+        quant_x(3)
+        layer1(3)
+        quant_h(1, 0, 256)
+        layer2(1, 0, 256)
+        y_out("s", 0, 0, 512)
+        quant_h(2, 0, 256)
+        layer2(2, 0, 256)
+        quant_h(3, 0, 128)
+        layer2(3, 0, 128)
+        quant_h(3, 128, 256)
+        layer2(3, 128, 256)
+        y_out("v", 0, 512, 1024)
+        y_out("s", 1, 0, 512)
+        y_out("s", 1, 512, 1024)
+
+        prod = [[keep.tile([P, V], F32, name=f"prod_{b}_{d}") for d in range(D)] for b in range(2)]
+        acc = [[keep.tile([P, V], F32, name=f"acc_{b}_{d}") for d in range(D - 1)] for b in range(2)]
+        for b in range(2):
+            for d in range(D):
+                nc.vector.tensor_tensor(out=prod[b][d][:], in0=y_sb[b][:].indirect(pos_sb[d][:]), in1=gates[b][:, d, :], op=MULT)
+                if d == 1:
+                    nc.vector.tensor_tensor(out=acc[b][0][:], in0=prod[b][0][:], in1=prod[b][1][:], op=ADD)
+                elif d > 1:
+                    nc.vector.tensor_tensor(out=acc[b][d - 1][:], in0=acc[b][d - 2][:], in1=prod[b][d][:], op=ADD)
+            nc.sync.dma_start(out=out[b * P : (b + 1) * P, :], in_=acc[b][D - 2][:])

@@ -1,6 +1,7 @@
 from contextlib import ExitStack
 
 import concourse.mybir as mybir
+from concourse.masks import make_identity
 
 K, T, D, S, V, H, N = 512, 2048, 4, 1024, 512, 512, 256
 FLOPS = 2 * S * (K * H + H * N) + 2 * D * N * V
@@ -31,19 +32,23 @@ def tile_picked_sub_mlp_gelu_sub_e_kernel(tc, xT, w1, w2, gate, offs, pos1, pos2
         nc.vector.memset(warm[:], 0.0)
         nc.scalar.activation(out=warm[:], in_=warm[:], func=GELU)
 
+        ident = keep.tile([P, P], F32, name="ident")
+        make_identity(nc, ident[:])
+
         w1_raw = keep.tile([P, 4, H], F32, name="w1_raw")
         w2_raw = keep.tile([P, 4, N], F32, name="w2_raw")
         x_view = xT.rearrange("(p u e) t -> u p e t", u=2, e=2)
-        chunks = ((0, 1024), (1024, 1024)), ((0, 1024), (1024, 512), (1536, 512))
+        chunks = ((0, 1024), (1024, 1024)), ((0, 1024), (1024, 768), (1792, 256))
         raws = []
         offs_sb = keep.tile([P, S // 16], U16, name="offs_sb")
         nc.sync.dma_start(offs_sb[:], offs)
-        nc.sync.dma_start(out=w1_raw[:], in_=w1.rearrange("(p j) c -> p j c", j=4))
         for u in range(2):
             for c0, n in chunks[u]:
                 raw = keep.tile([P, 2, n], F32, name=f"x_raw_{u}_{c0}")
                 nc.sync.dma_start(out=raw[:], in_=x_view[u, :, :, c0 : c0 + n])
                 raws.append((u, c0, n, raw))
+                if (u, c0) == (1, 0):
+                    nc.sync.dma_start(out=w1_raw[:], in_=w1.rearrange("(p j) c -> p j c", j=4))
         nc.sync.dma_start(out=w2_raw[:], in_=w2.rearrange("(p j) c -> p j c", j=4))
         pos_sb = []
         for d, pos in enumerate((pos1, pos2, pos3, pos4)):
@@ -80,8 +85,9 @@ def tile_picked_sub_mlp_gelu_sub_e_kernel(tc, xT, w1, w2, gate, offs, pos1, pos2
             nc.vector.tensor_copy(out=words[:, :, u], in_=window.indirect(offs_sb[:, i * cols : (i + 1) * cols]))
 
         for u, c0, n, raw in raws:
-            v_share = 384 if n == 1024 else (128 if c0 == 1024 else 320)
-            cast("s", u, c0, raw, v_share, n)
+            v_share = {1024: 576, 768: 448, 256: 256}[n]
+            if v_share < n:
+                cast("s", u, c0, raw, v_share, n)
             cast("v", u, c0, raw, 0, v_share)
             if u == 0 and c0 + n == T:
                 for i in range(S // SLICE):
@@ -104,7 +110,7 @@ def tile_picked_sub_mlp_gelu_sub_e_kernel(tc, xT, w1, w2, gate, offs, pos1, pos2
         def layer1(i):
             for half in range(SLICE // P):
                 cols = slice(half * P, (half + 1) * P)
-                ps = psum_h.tile([P, 4, P], F32, name="ps_h")
+                ps = psum_h.tile([P, 4, P], F32, tag="ps_h", name="ps_h")
                 for t in range(4):
                     nc.tensor.matmul_mx(
                         out=ps[:, t, :],
@@ -142,17 +148,17 @@ def tile_picked_sub_mlp_gelu_sub_e_kernel(tc, xT, w1, w2, gate, offs, pos1, pos2
             else:
                 nc.scalar.activation(out=o, in_=i, func=COPY)
 
+        nc.gpsimd.tensor_scalar(out=w2_bf[:], in0=w2_raw[:].rearrange("p j c -> p c j"), scalar1=1.0, scalar2=0.0, op0=MULT, op1=ADD)
         gather(1, 0)
         quant_x(0)
         layer1(0)
         gather(1, 1)
         quant_x(1)
         layer1(1)
-        nc.vector.tensor_copy(out=w2_bf[:], in_=w2_raw[:].rearrange("p j c -> p c j"))
-        nc.vector.quantize_mx(out=w2_q[:].bitcast(FP8X4), scales=w2_s[:], in_=w2_bf[:].rearrange("p c j -> p (c j)"))
         gather(1, 2)
         quant_x(2)
         layer1(2)
+        nc.vector.quantize_mx(out=w2_q[:].bitcast(FP8X4), scales=w2_s[:], in_=w2_bf[:].rearrange("p c j -> p (c j)"))
         quant_h(0, 0, 256)
         layer2(0, 0, 256)
         gather(1, 3)
@@ -163,21 +169,58 @@ def tile_picked_sub_mlp_gelu_sub_e_kernel(tc, xT, w1, w2, gate, offs, pos1, pos2
         y_out("s", 0, 0, 512)
         quant_h(2, 0, 256)
         layer2(2, 0, 256)
+        y_out("v", 1, 0, 512)
         quant_h(3, 0, 128)
         layer2(3, 0, 128)
         quant_h(3, 128, 256)
         layer2(3, 128, 256)
         y_out("v", 0, 512, 1024)
-        y_out("s", 1, 0, 512)
         y_out("s", 1, 512, 1024)
 
         prod = [[keep.tile([P, V], F32, name=f"prod_{b}_{d}") for d in range(D)] for b in range(2)]
-        acc = [[keep.tile([P, V], F32, name=f"acc_{b}_{d}") for d in range(D - 1)] for b in range(2)]
-        for b in range(2):
-            for d in range(D):
-                nc.vector.tensor_tensor(out=prod[b][d][:], in0=y_sb[b][:].indirect(pos_sb[d][:]), in1=gates[b][:, d, :], op=MULT)
-                if d == 1:
-                    nc.vector.tensor_tensor(out=acc[b][0][:], in0=prod[b][0][:], in1=prod[b][1][:], op=ADD)
-                elif d > 1:
-                    nc.vector.tensor_tensor(out=acc[b][d - 1][:], in0=acc[b][d - 2][:], in1=prod[b][d][:], op=ADD)
-            nc.sync.dma_start(out=out[b * P : (b + 1) * P, :], in_=acc[b][D - 2][:])
+
+        def neighbour(b, d):
+            nc.vector.tensor_tensor(out=prod[b][d][:], in0=y_sb[b][:].indirect(pos_sb[d][:]), in1=gates[b][:, d, :], op=MULT)
+
+        def turn_add(b, d, banks, last):
+            per = 4 // len(banks)
+            for k in range(4):
+                nc.tensor.matmul(
+                    out=banks[k // per][:, k % per, :],
+                    lhsT=prod[b][d][:, k * P : (k + 1) * P],
+                    rhs=ident[:],
+                    is_transpose=True,
+                    start=(d == 0 and k % per == 0),
+                    stop=(d == last and k % per == per - 1),
+                )
+
+        def turn_back(banks, back, turned):
+            per = 4 // len(banks)
+            for i in range(len(banks)):
+                nc.scalar.activation(out=turned[:, i * per : (i + 1) * per, :], in_=banks[i][:, 0:per, :], func=COPY)
+                for k in range(i * per, (i + 1) * per):
+                    nc.tensor.transpose(back[:, k, :], turned[:, k, :], ident[:])
+
+        result = [keep.tile([P, V], F32, name=f"result_{b}") for b in range(2)]
+        turned = [keep.tile([P, 4, P], F32, name=f"turned_{b}") for b in range(2)]
+
+        sums0 = psum_h.tile([P, 4, P], F32, tag="ps_h", name="sums0")
+        for d in range(D):
+            neighbour(0, d)
+            turn_add(0, d, [sums0], D - 1)
+        back0 = psum_h.tile([P, 4, P], F32, tag="ps_h", name="back0")
+        turn_back([sums0], back0, turned[0])
+        nc.scalar.activation(out=result[0][:], in_=back0[:].rearrange("p k n -> p (k n)"), func=COPY)
+        nc.sync.dma_start(out=out[0:P, :], in_=result[0][:])
+
+        sums1 = [psum_h.tile([P, 4, P], F32, tag="ps_h", name=f"sums1_{i}") for i in range(2)]
+        for d in range(D - 1):
+            neighbour(1, d)
+            turn_add(1, d, sums1, D - 2)
+        neighbour(1, D - 1)
+        back1 = psum_h.tile([P, 4, P], F32, tag="ps_h", name="back1")
+        turn_back(sums1, back1, turned[1])
+        for a in range(2):
+            c = slice(a * 256, (a + 1) * 256)
+            nc.vector.tensor_tensor(out=result[1][:, c], in0=back1[:].rearrange("p k n -> p (k n)")[:, c], in1=prod[1][D - 1][:, c], op=ADD)
+            nc.sync.dma_start(out=out[P : 2 * P, c], in_=result[1][:, c])

@@ -42,13 +42,12 @@ def tile_picked_sub_mlp_gelu_sub_e_kernel(tc, xT, w1, w2, gate, offs, pos1, pos2
         raws = []
         offs_sb = keep.tile([P, S // 16], U16, name="offs_sb")
         nc.sync.dma_start(offs_sb[:], offs)
+        nc.sync.dma_start(out=w1_raw[:], in_=w1.rearrange("(p j) c -> p j c", j=4))
         for u in range(2):
             for c0, n in chunks[u]:
                 raw = keep.tile([P, 2, n], F32, name=f"x_raw_{u}_{c0}")
                 nc.sync.dma_start(out=raw[:], in_=x_view[u, :, :, c0 : c0 + n])
                 raws.append((u, c0, n, raw))
-                if (u, c0) == (1, 0):
-                    nc.sync.dma_start(out=w1_raw[:], in_=w1.rearrange("(p j) c -> p j c", j=4))
         nc.sync.dma_start(out=w2_raw[:], in_=w2.rearrange("(p j) c -> p j c", j=4))
         pos_sb = []
         for d, pos in enumerate((pos1, pos2, pos3, pos4)):
@@ -148,7 +147,7 @@ def tile_picked_sub_mlp_gelu_sub_e_kernel(tc, xT, w1, w2, gate, offs, pos1, pos2
             else:
                 nc.scalar.activation(out=o, in_=i, func=COPY)
 
-        nc.gpsimd.tensor_scalar(out=w2_bf[:], in0=w2_raw[:].rearrange("p j c -> p c j"), scalar1=1.0, scalar2=0.0, op0=MULT, op1=ADD)
+        nc.scalar.activation(out=w2_bf[:], in_=w2_raw[:].rearrange("p j c -> p c j"), func=COPY)
         gather(1, 0)
         quant_x(0)
         layer1(0)
@@ -169,12 +168,13 @@ def tile_picked_sub_mlp_gelu_sub_e_kernel(tc, xT, w1, w2, gate, offs, pos1, pos2
         y_out("s", 0, 0, 512)
         quant_h(2, 0, 256)
         layer2(2, 0, 256)
-        y_out("v", 1, 0, 512)
+        y_out("v", 0, 512, 768)
         quant_h(3, 0, 128)
         layer2(3, 0, 128)
         quant_h(3, 128, 256)
         layer2(3, 128, 256)
-        y_out("v", 0, 512, 1024)
+        y_out("v", 0, 768, 1024)
+        y_out("s", 1, 0, 512)
         y_out("s", 1, 512, 1024)
 
         prod = [[keep.tile([P, V], F32, name=f"prod_{b}_{d}") for d in range(D)] for b in range(2)]
@@ -204,23 +204,21 @@ def tile_picked_sub_mlp_gelu_sub_e_kernel(tc, xT, w1, w2, gate, offs, pos1, pos2
         result = [keep.tile([P, V], F32, name=f"result_{b}") for b in range(2)]
         turned = [keep.tile([P, 4, P], F32, name=f"turned_{b}") for b in range(2)]
 
-        sums0 = psum_h.tile([P, 4, P], F32, tag="ps_h", name="sums0")
-        for d in range(D):
-            neighbour(0, d)
-            turn_add(0, d, [sums0], D - 1)
-        back0 = psum_h.tile([P, 4, P], F32, tag="ps_h", name="back0")
-        turn_back([sums0], back0, turned[0])
-        nc.scalar.activation(out=result[0][:], in_=back0[:].rearrange("p k n -> p (k n)"), func=COPY)
-        nc.sync.dma_start(out=out[0:P, :], in_=result[0][:])
-
-        sums1 = [psum_h.tile([P, 4, P], F32, tag="ps_h", name=f"sums1_{i}") for i in range(2)]
-        for d in range(D - 1):
-            neighbour(1, d)
-            turn_add(1, d, sums1, D - 2)
+        back = []
+        for b in range(2):
+            sums = psum_h.tile([P, 4, P], F32, tag="ps_h", name=f"sums_{b}")
+            for d in range(D - 1):
+                neighbour(b, d)
+                turn_add(b, d, [sums], D - 2)
+            back.append(psum_h.tile([P, 4, P], F32, tag="ps_h", name=f"back_{b}"))
+            turn_back([sums], back[b], turned[b])
+        neighbour(0, D - 1)
         neighbour(1, D - 1)
-        back1 = psum_h.tile([P, 4, P], F32, tag="ps_h", name="back1")
-        turn_back(sums1, back1, turned[1])
-        for a in range(2):
-            c = slice(a * 256, (a + 1) * 256)
-            nc.vector.tensor_tensor(out=result[1][:, c], in0=back1[:].rearrange("p k n -> p (k n)")[:, c], in1=prod[1][D - 1][:, c], op=ADD)
-            nc.sync.dma_start(out=out[P : 2 * P, c], in_=result[1][:, c])
+
+        def last_add(b, c):
+            nc.vector.tensor_tensor(out=result[b][:, c], in0=back[b][:].rearrange("p k n -> p (k n)")[:, c], in1=prod[b][D - 1][:, c], op=ADD)
+            nc.sync.dma_start(out=out[b * P : (b + 1) * P, c], in_=result[b][:, c])
+
+        last_add(0, slice(0, 512))
+        last_add(1, slice(0, 256))
+        last_add(1, slice(256, 512))

@@ -38,7 +38,7 @@ def tile_picked_sub_mlp_gelu_sub_e_kernel(tc, xT, w1, w2, gate, offs, pos1, pos2
         w1_raw = keep.tile([P, 4, H], F32, name="w1_raw")
         w2_raw = keep.tile([P, 4, N], F32, name="w2_raw")
         x_view = xT.rearrange("(p u e) t -> u p e t", u=2, e=2)
-        chunks = ((0, 1024), (1024, 1024)), ((0, 1024), (1024, 768), (1792, 256))
+        chunks = [[(c0, 512) for c0 in range(0, T, 512)] for u in range(2)]
         raws = []
         offs_sb = keep.tile([P, S // 16], U16, name="offs_sb")
         nc.sync.dma_start(offs_sb[:], offs)
@@ -84,10 +84,10 @@ def tile_picked_sub_mlp_gelu_sub_e_kernel(tc, xT, w1, w2, gate, offs, pos1, pos2
             nc.vector.tensor_copy(out=words[:, :, u], in_=window.indirect(offs_sb[:, i * cols : (i + 1) * cols]))
 
         for u, c0, n, raw in raws:
-            v_share = {1024: 576, 768: 448, 256: 256}[n]
-            if v_share < n:
-                cast("s", u, c0, raw, v_share, n)
-            cast("v", u, c0, raw, 0, v_share)
+            v_share = (384, 384, 384, 320, 0, 0, 192, 320)[u * 4 + c0 // 512]
+            cast("s", u, c0, raw, v_share, n)
+            if v_share > 0:
+                cast("v", u, c0, raw, 0, v_share)
             if u == 0 and c0 + n == T:
                 for i in range(S // SLICE):
                     gather(0, i)
@@ -168,7 +168,7 @@ def tile_picked_sub_mlp_gelu_sub_e_kernel(tc, xT, w1, w2, gate, offs, pos1, pos2
         y_out("s", 0, 0, 512)
         quant_h(2, 0, 256)
         layer2(2, 0, 256)
-        y_out("v", 0, 512, 768)
+        y_out("s", 0, 512, 768)
         quant_h(3, 0, 128)
         layer2(3, 0, 128)
         quant_h(3, 128, 256)

from contextlib import ExitStack

import concourse.mybir as mybir
from concourse.masks import make_identity

K, T, D, S, V, H, N = 512, 2048, 4, 1024, 512, 512, 256
FLOPS = 2 * S * (K * H + H * N) + 2 * D * N * V

F32 = mybir.dt.float32
BF16 = mybir.dt.bfloat16
U32 = mybir.dt.uint32
U16 = mybir.dt.uint16
U8 = mybir.dt.uint8
FP8X4 = mybir.dt.float8_e4m3fn_x4
COPY = mybir.ActivationFunctionType.Copy
GELU = mybir.ActivationFunctionType.Gelu_apprx_tanh
MULT = mybir.AluOpType.mult
ADD = mybir.AluOpType.add

P = 128
SLICE = 256


def tile_picked_sub_mlp_gelu_sub_e_kernel(tc, xT, w1, w2, gate, offs, pos1, pos2, pos3, pos4, out):
    nc = tc.nc
    with ExitStack() as ctx:
        keep = ctx.enter_context(tc.tile_pool(name="keep", bufs=1))
        psum_h = ctx.enter_context(tc.psum_pool(name="psum_h", bufs=4))
        psum_y = ctx.enter_context(tc.psum_pool(name="psum_y", bufs=1))

        warm = keep.tile([P, 1], F32, name="warm")
        nc.vector.memset(warm[:], 0.0)
        nc.scalar.activation(out=warm[:], in_=warm[:], func=GELU)

        ident = keep.tile([P, P], F32, name="ident")
        make_identity(nc, ident[:])

        w1_raw = keep.tile([P, 4, H], F32, name="w1_raw")
        w2_raw = keep.tile([P, 4, N], F32, name="w2_raw")
        x_view = xT.rearrange("(p u e) t -> u p e t", u=2, e=2)
        chunks = [[(c0, 512) for c0 in range(0, T, 512)] for u in range(2)]
        raws = []
        offs_sb = keep.tile([P, S // 16], U16, name="offs_sb")
        nc.sync.dma_start(offs_sb[:], offs)
        nc.sync.dma_start(out=w1_raw[:], in_=w1.rearrange("(p j) c -> p j c", j=4))
        for u in range(2):
            for c0, n in chunks[u]:
                raw = keep.tile([P, 2, n], F32, name=f"x_raw_{u}_{c0}")
                nc.sync.dma_start(out=raw[:], in_=x_view[u, :, :, c0 : c0 + n])
                raws.append((u, c0, n, raw))
        nc.sync.dma_start(out=w2_raw[:], in_=w2.rearrange("(p j) c -> p j c", j=4))
        pos_sb = []
        for d, pos in enumerate((pos1, pos2, pos3, pos4)):
            t = keep.tile([P, V // 16], U16, name=f"pos_sb_{d}")
            nc.sync.dma_start(t[:], pos)
            pos_sb.append(t)
        gates = []
        for b in range(2):
            t = keep.tile([P, D, V], F32, name=f"gate_sb_{b}")
            nc.sync.dma_start(out=t[:], in_=gate[:, b * P : (b + 1) * P, :].rearrange("d p v -> p d v"))
            gates.append(t)

        w1_bf = keep.tile([P, 4, P, 4], BF16, align_bytes=64, name="w1_bf")
        w1_q = keep.tile([P, H], U32, align_bytes=64, name="w1_q")
        w1_s = keep.tile([P, H], U8, align_bytes=64, name="w1_s")
        nc.vector.tensor_copy(out=w1_bf[:], in_=w1_raw[:].rearrange("p j (m t) -> p t m j", t=4))
        nc.vector.quantize_mx(out=w1_q[:].bitcast(FP8X4), scales=w1_s[:], in_=w1_bf[:].rearrange("p t m j -> p (t m j)"))

        pairs = [keep.tile([P, T, 2], BF16, align_bytes=64, name=f"pair_{u}") for u in range(2)]
        picked = [keep.tile([P, SLICE, 4], BF16, align_bytes=64, name=f"picked_{i}") for i in range(S // SLICE)]

        def cast(engine, u, c0, raw, a, b):
            o = pairs[u][:, c0 + a : c0 + b, :]
            i = raw[:, :, a:b].rearrange("p e t -> p t e")
            if engine == "v":
                nc.vector.tensor_copy(out=o, in_=i)
            else:
                nc.scalar.activation(out=o, in_=i, func=COPY)

        def gather(u, i):
            words = picked[i][:].rearrange("p n k -> p (n k)").bitcast(U32).rearrange("p (n u) -> p n u", u=2)
            window = pairs[u][:].rearrange("p t e -> p (t e)").bitcast(U32)
            cols = SLICE // 16
            nc.vector.tensor_copy(out=words[:, :, u], in_=window.indirect(offs_sb[:, i * cols : (i + 1) * cols]))

        for u, c0, n, raw in raws:
            v_share = (384, 384, 384, 320, 0, 0, 192, 320)[u * 4 + c0 // 512]
            cast("s", u, c0, raw, v_share, n)
            if v_share > 0:
                cast("v", u, c0, raw, 0, v_share)
            if u == 0 and c0 + n == T:
                for i in range(S // SLICE):
                    gather(0, i)

        x_q = [keep.tile([P, SLICE], U32, align_bytes=64, name=f"x_q_{i}") for i in range(S // SLICE)]
        x_s = [keep.tile([P, SLICE], U8, align_bytes=64, name=f"x_s_{i}") for i in range(S // SLICE)]
        h_bf = [keep.tile([P, SLICE, 4], BF16, align_bytes=64, name=f"h_bf_{i}") for i in range(S // SLICE)]
        h_q = [keep.tile([P, SLICE], U32, align_bytes=64, name=f"h_q_{i}") for i in range(S // SLICE)]
        h_s = [keep.tile([P, SLICE], U8, align_bytes=64, name=f"h_s_{i}") for i in range(S // SLICE)]
        w2_bf = keep.tile([P, N, 4], BF16, align_bytes=64, name="w2_bf")
        w2_q = keep.tile([P, N], U32, align_bytes=64, name="w2_q")
        w2_s = keep.tile([P, N], U8, align_bytes=64, name="w2_s")
        y_ps = [[psum_y.tile([P, 512], F32, name=f"y_ps_{b}_{i}") for i in range(2)] for b in range(2)]
        y_sb = [keep.tile([P, S], F32, name=f"y_sb_{b}") for b in range(2)]

        def quant_x(i):
            nc.vector.quantize_mx(out=x_q[i][:].bitcast(FP8X4), scales=x_s[i][:], in_=picked[i][:].rearrange("p n k -> p (n k)"))

        def layer1(i):
            for half in range(SLICE // P):
                cols = slice(half * P, (half + 1) * P)
                ps = psum_h.tile([P, 4, P], F32, tag="ps_h", name="ps_h")
                for t in range(4):
                    nc.tensor.matmul_mx(
                        out=ps[:, t, :],
                        lhsT=w1_q[:, t * P : (t + 1) * P].bitcast(FP8X4),
                        lhsT_scale=w1_s[:, t * P : (t + 1) * P],
                        rhs=x_q[i][:, cols].bitcast(FP8X4),
                        rhs_scale=x_s[i][:, cols],
                        start=True,
                        stop=True,
                    )
                nc.scalar.activation(out=h_bf[i][:, cols, :], in_=ps[:].rearrange("p t n -> p n t"), func=GELU)

        def quant_h(i, a, b):
            nc.vector.quantize_mx(
                out=h_q[i][:, a:b].bitcast(FP8X4), scales=h_s[i][:, a:b], in_=h_bf[i][:, a:b, :].rearrange("p n k -> p (n k)")
            )

        def layer2(i, a, b):
            for m in range(2):
                c = (i % 2) * SLICE
                nc.tensor.matmul_mx(
                    out=y_ps[m][i // 2][:, c + a : c + b],
                    lhsT=w2_q[:, m * P : (m + 1) * P].bitcast(FP8X4),
                    lhsT_scale=w2_s[:, m * P : (m + 1) * P],
                    rhs=h_q[i][:, a:b].bitcast(FP8X4),
                    rhs_scale=h_s[i][:, a:b],
                    start=True,
                    stop=True,
                )

        def y_out(engine, m, a, b):
            o, i = y_sb[m][:, a:b], y_ps[m][a // 512][:, a % 512 : (b - 1) % 512 + 1]
            if engine == "v":
                nc.vector.tensor_copy(out=o, in_=i)
            else:
                nc.scalar.activation(out=o, in_=i, func=COPY)

        nc.scalar.activation(out=w2_bf[:], in_=w2_raw[:].rearrange("p j c -> p c j"), func=COPY)
        gather(1, 0)
        quant_x(0)
        layer1(0)
        gather(1, 1)
        quant_x(1)
        layer1(1)
        gather(1, 2)
        quant_x(2)
        layer1(2)
        nc.vector.quantize_mx(out=w2_q[:].bitcast(FP8X4), scales=w2_s[:], in_=w2_bf[:].rearrange("p c j -> p (c j)"))
        quant_h(0, 0, 256)
        layer2(0, 0, 256)
        gather(1, 3)
        quant_x(3)
        layer1(3)
        quant_h(1, 0, 256)
        layer2(1, 0, 256)
        y_out("s", 0, 0, 512)
        quant_h(2, 0, 256)
        layer2(2, 0, 256)
        y_out("s", 0, 512, 768)
        quant_h(3, 0, 128)
        layer2(3, 0, 128)
        quant_h(3, 128, 256)
        layer2(3, 128, 256)
        y_out("v", 0, 768, 1024)
        y_out("s", 1, 0, 512)
        y_out("s", 1, 512, 1024)

        prod = [[keep.tile([P, V], F32, name=f"prod_{b}_{d}") for d in range(D)] for b in range(2)]

        def neighbour(b, d):
            nc.vector.tensor_tensor(out=prod[b][d][:], in0=y_sb[b][:].indirect(pos_sb[d][:]), in1=gates[b][:, d, :], op=MULT)

        def turn_add(b, d, banks, last):
            per = 4 // len(banks)
            for k in range(4):
                nc.tensor.matmul(
                    out=banks[k // per][:, k % per, :],
                    lhsT=prod[b][d][:, k * P : (k + 1) * P],
                    rhs=ident[:],
                    is_transpose=True,
                    start=(d == 0 and k % per == 0),
                    stop=(d == last and k % per == per - 1),
                )

        def turn_back(banks, back, turned):
            per = 4 // len(banks)
            for i in range(len(banks)):
                nc.scalar.activation(out=turned[:, i * per : (i + 1) * per, :], in_=banks[i][:, 0:per, :], func=COPY)
                for k in range(i * per, (i + 1) * per):
                    nc.tensor.transpose(back[:, k, :], turned[:, k, :], ident[:])

        result = [keep.tile([P, V], F32, name=f"result_{b}") for b in range(2)]
        turned = [keep.tile([P, 4, P], F32, name=f"turned_{b}") for b in range(2)]

        back = []
        for b in range(2):
            sums = psum_h.tile([P, 4, P], F32, tag="ps_h", name=f"sums_{b}")
            for d in range(D - 1):
                neighbour(b, d)
                turn_add(b, d, [sums], D - 2)
            back.append(psum_h.tile([P, 4, P], F32, tag="ps_h", name=f"back_{b}"))
            turn_back([sums], back[b], turned[b])
        neighbour(0, D - 1)
        neighbour(1, D - 1)

        def last_add(b, c):
            nc.vector.tensor_tensor(out=result[b][:, c], in0=back[b][:].rearrange("p k n -> p (k n)")[:, c], in1=prod[b][D - 1][:, c], op=ADD)
            nc.sync.dma_start(out=out[b * P : (b + 1) * P, c], in_=result[b][:, c])

        last_add(0, slice(0, 512))
        last_add(1, slice(0, 256))
        last_add(1, slice(256, 512))
